import numpy as np
import ml_dtypes


def mxq(x, axis, fmt="e4m3"):
    dtype, down = {"e4m3": (ml_dtypes.float8_e4m3fn, 7), "e5m2": (ml_dtypes.float8_e5m2, 14)}[fmt]
    v = np.moveaxis(np.asarray(x, np.float32).astype(ml_dtypes.bfloat16).astype(np.float64), axis, -1)
    blocks = v.reshape(v.shape[:-1] + (-1, 32))
    amax = np.abs(blocks).max(-1, keepdims=True)
    byte = np.maximum(np.where(amax > 0, np.frexp(amax)[1] - 1 + 127, 0) - down, 1)
    scale = np.exp2(byte - 127.0)
    codes = (blocks / scale).astype(np.float32).astype(dtype).astype(np.float64)
    return np.moveaxis((codes * scale).reshape(v.shape), -1, axis)


WIDE = False


def mx_kscale(k):
    if not WIDE:
        return np.ones(k)
    levels = np.array([10, -10, 5, -5, 0])
    if k % 512:
        return np.exp2(np.random.permutation(np.resize(levels, k // 32))).repeat(32)
    a = np.empty((k // 512, 16))
    for p in range(k // 512):
        a[p, :8] = np.random.permutation(np.resize(levels, 8))
        for g in range(8):
            far = levels[np.abs(levels - a[p, g]) >= 10]
            a[p, g + 8] = far[np.random.randint(len(far))]
    return np.exp2(a.ravel()).repeat(32)


BF16 = ml_dtypes.bfloat16


def bf(x):
    return np.asarray(x, np.float32).astype(BF16)


def f64(x):
    return np.asarray(x).astype(np.float64)


E2M1 = np.array([0.0, 0.5, 1.0, 1.5, 2.0, 3.0, 4.0, 6.0, -0.0, -0.5, -1.0, -1.5, -2.0, -3.0, -4.0, -6.0])


def pack_weight(w, fmt):
    k, n = w.shape
    w = f64(bf(w)).reshape(k // 32, 32, n)
    amax = np.abs(w).max(1)
    if fmt == "e4m3":
        byte = np.frexp(amax)[1] - 1 + 127 - 7
    else:
        mant, ex = np.frexp(amax / 6.0)
        byte = np.where(mant > 0.5, ex, ex - 1) + 127
    byte = np.clip(np.where(amax > 0, byte, 1), 1, 254)
    scaled = (w * np.exp2(127.0 - byte)[:, None, :]).reshape(k, n).astype(np.float32)
    by_word = np.ascontiguousarray(scaled.reshape(k // 512, 128, 4, n).transpose(0, 1, 3, 2))
    if fmt == "e4m3":
        words = by_word.astype(ml_dtypes.float8_e4m3fn).view(np.uint8)
    else:
        c = by_word.astype(ml_dtypes.float4_e2m1fn).view(np.uint8) & 0xF
        words = c[..., 0::2] | (c[..., 1::2] << 4)
    return np.ascontiguousarray(words), np.ascontiguousarray(byte.astype(np.uint8).reshape(k // 512, 16, n))


def unpack_weight(words, scales, fmt):
    g, p, n, _ = words.shape
    if fmt == "e4m3":
        vals = np.ascontiguousarray(words).view(ml_dtypes.float8_e4m3fn).astype(np.float64)
    else:
        nib = np.empty((g, p, n, 4), np.uint8)
        nib[..., 0::2] = words & 0xF
        nib[..., 1::2] = words >> 4
        vals = E2M1[nib]
    vals = vals * np.repeat(np.exp2(scales.astype(np.float64) - 127.0), 8, axis=1)[..., None]
    return vals.transpose(0, 1, 3, 2).reshape(g * 512, n)
def pack4(w):
    words, scales = pack_weight(w, "e2m1")
    return words.reshape(words.shape[0], 128, -1), scales


def unpack4(words, scales):
    return unpack_weight(words.reshape(words.shape[0], 128, -1, 2), scales, "e2m1")


N, C = 1024, 512

A_STD = 0.5
Y_STD = 2.0


def setup_inputs():
    s, r = mx_kscale(N), mx_kscale(N)
    finv = np.random.standard_normal((N, N)) / np.sqrt(N) * s
    a = A_STD * np.random.standard_normal((N, N)) / s[:, None] / s
    c = (1 + 0.1 * np.random.standard_normal(N)) * r
    w = (1 + 0.1 * np.random.standard_normal(N)) / r
    y = Y_STD * np.random.standard_normal((N, C)) / np.sqrt(N) / r[:, None]
    y_words, y_scales = pack4(y)
    return {"finv": bf(finv), "a": bf(a), "c": bf(c), "w": bf(w),
            "y_words": y_words, "y_scales": y_scales}


def reference(finv, a, c, w, y_words, y_scales):
    fq = mxq(f64(finv), 1, "e4m3")
    h = (mxq(f64(a), 1, "e4m3") @ fq.T) * f64(c)
    e = (fq @ mxq(h, 0, "e4m3")) * f64(w) - np.eye(N)
    v = mxq(h, 1, "e4m3") @ unpack4(y_words, y_scales)
    return e, v

@@ -1,0 +1,343 @@
+from contextlib import ExitStack
+
+import concourse.mybir as mybir
+from concourse.masks import make_identity
+
+N, C = 1024, 512
+FLOPS = 2 * N * N * N * 2 + 2 * N * N * C
+
+F32 = mybir.dt.float32
+BF16 = mybir.dt.bfloat16
+U32 = mybir.dt.uint32
+I32 = mybir.dt.int32
+U8 = mybir.dt.uint8
+FP8X4 = mybir.dt.float8_e4m3fn_x4
+FP4X4 = mybir.dt.float4_e2m1fn_x4
+ALU = mybir.AluOpType
+ACT = mybir.ActivationFunctionType
+
+P = 128
+PACK = 4
+G = 512
+BANKS = 8
+
+
+def tile_split_preconditioned_operator_s8_kernel(tc, finv, a, c, w, y_words, y_scales, out_0, out_1):
+    nc = tc.nc
+    with ExitStack() as ctx:
+        keep = ctx.enter_context(tc.tile_pool(name="keep", bufs=1))
+        ring = ctx.enter_context(tc.tile_pool(name="ring", bufs=4))
+        psum = ctx.enter_context(tc.psum_pool(name="psum", bufs=1))
+        ctx.enter_context(tc.manual_schedule())
+
+        used = [0]
+
+        def new_bank():
+            n = used.pop()
+            used.append(n + 1)
+            return psum.tile([P, G], F32, name="bank%d" % (n % BANKS))
+
+        def planes(name, width):
+            codes = keep.tile([P, width], U32, name=name + "_codes", align_bytes=64)
+            scales = keep.tile([P, width], U8, name=name + "_scales", align_bytes=64)
+            return codes, scales
+
+        src = {"a": a, "f": finv}
+        raw = {}
+
+        def load(x, g, t0, nt):
+            tile = keep.tile([P, nt * N], BF16, name="raw_%s%d%d" % (x, g, t0), align_bytes=64)
+            rows = src[x].rearrange("(g m t) k -> g m (t k)", g=2, t=PACK)
+            nc.sync.dma_start(out=tile[:], in_=rows[g, :, t0 * N : (t0 + nt) * N])
+            for t in range(nt):
+                raw[x, g, t0 + t] = tile[:, t * N : (t + 1) * N].bitcast(F32)
+
+        ident = keep.tile([P, P], F32, name="ident")
+        make_identity(nc, ident[:])
+        c_bf = keep.tile([P, 2, PACK], BF16, name="c_bf")
+        c_f32 = keep.tile([P, 2, PACK], F32, name="c_f32")
+        w_all = keep.tile([P, N], BF16, name="w_all")
+        y_codes = keep.tile([P, 2, 2 * C], U8, name="y_codes", align_bytes=64)
+        y_sc = keep.tile([P, 2, C], U8, name="y_sc", align_bytes=64)
+        nc.vector.memset(y_sc[:].bitcast(I32), 0)
+
+        nc.scalar.dma_start(out=c_bf[:], in_=c.rearrange("(g p t) -> p g t", g=2, t=PACK))
+        for t in range(PACK):
+            load("a", 0, t, 1)
+        for t in range(PACK):
+            load("f", 0, t, 1)
+        for x in ("a", "f"):
+            load(x, 1, 0, 2)
+            load(x, 1, 2, 2)
+        nc.sync.dma_start(out=w_all[:], in_=w.partition_broadcast(P))
+        nc.sync.dma_start(out=y_codes[:].bitcast(I32), in_=y_words.rearrange("g p n -> p g n").bitcast(I32))
+        for q in range(4):
+            nc.sync.dma_start(
+                out=y_sc[32 * q : 32 * q + 4].bitcast(I32),
+                in_=y_scales[:, 4 * q : 4 * q + 4, :].rearrange("g r n -> r g n").bitcast(I32),
+            )
+        nc.vector.tensor_copy(out=c_f32[:], in_=c_bf[:])
+
+        fq = {(g, t): planes("fq%d%d" % (g, t), 2 * P) for g in range(2) for t in range(PACK)}
+        aq = {(g, kg): planes("aq%d%d" % (g, kg), G) for g in range(2) for kg in range(2)}
+        h0q = {(g, gr): planes("h0q%d%d" % (g, gr), G) for g in range(2) for gr in range(2)}
+        h1q = {(g, gr): planes("h1q%d%d" % (g, gr), G) for g in range(2) for gr in range(2)}
+        ht = {(g, gr): keep.tile([P, PACK * G], BF16, name="ht%d%d" % (g, gr), align_bytes=64) for g in range(2) for gr in range(2)}
+        live = {}
+
+        def copy_on(eng, out, in_):
+            if eng == "s":
+                nc.scalar.copy(out=out, in_=in_)
+            else:
+                nc.vector.tensor_copy(out=out, in_=in_)
+
+        def quantize(dst, cols, in_):
+            nc.vector.quantize_mx(out=dst[0][:, cols].bitcast(FP8X4), scales=dst[1][:, cols], in_=in_)
+
+        def sort_words(x, g, t):
+            tile = ring.tile([P, G], F32, name="sorted", align_bytes=64)
+            nc.vector.tensor_copy(
+                out=tile[:].rearrange("m (kg u p) -> m kg u p", kg=2, u=2),
+                in_=raw[x, g, t].rearrange("m (kg p u) -> m kg u p", kg=2, u=2),
+            )
+            live["sorted", x, g, t] = tile
+
+        def turn(x, g, t):
+            bank = new_bank()
+            for kg in range(2):
+                for u in range(2):
+                    s = 2 * kg + u
+                    if ("sorted", x, g, t) in live:
+                        words = live["sorted", x, g, t][:, s * P : (s + 1) * P]
+                    else:
+                        words = raw[x, g, t][:, 256 * kg + u : 256 * (kg + 1) : 2]
+                    nc.tensor.transpose(bank[:, s * P : (s + 1) * P], words, ident[:])
+            live["bank", x, g, t] = bank
+
+        def turn_out(x, g, t, eng):
+            stage = ring.tile([P, N], BF16, name="stage", align_bytes=64)
+            copy_on(
+                eng,
+                stage[:].bitcast(F32).rearrange("p (kg m u) -> p kg m u", kg=2, u=2),
+                live["bank", x, g, t][:].rearrange("p (kg u m) -> p kg m u", kg=2, u=2),
+            )
+            live["stage", x, g, t] = stage
+
+        def turn_q(x, g, t):
+            stage = live["stage", x, g, t]
+            if x == "f":
+                quantize(fq[g, t], slice(0, 2 * P), stage[:])
+            else:
+                for kg in range(2):
+                    quantize(aq[g, kg], slice(t * P, (t + 1) * P), stage[:, kg * G : (kg + 1) * G])
+
+        def mx(bank, lhs, rhs):
+            for kg in range(2):
+                nc.tensor.matmul_mx(
+                    out=bank[:], lhsT=lhs[kg][0], lhsT_scale=lhs[kg][1], rhs=rhs[kg][0], rhs_scale=rhs[kg][1],
+                    start=(kg == 0), stop=(kg == 1),
+                )
+
+        def fp8(pl, cols):
+            return pl[0][:, cols].bitcast(FP8X4), pl[1][:, cols]
+
+        def f_cols(g, t):
+            return [fp8(fq[g, t], slice(kg * P, (kg + 1) * P)) for kg in range(2)]
+
+        def h_mm(g, t, gr):
+            bank = new_bank()
+            mx(bank, f_cols(g, t), [fp8(aq[gr, kg], slice(0, G)) for kg in range(2)])
+            live["h", g, t, gr] = bank
+
+        def h_out(g, t, gr, eng):
+            out = ht[g, gr][:, t * G : (t + 1) * G].rearrange("p (u m e) -> p u m e", u=2, e=2)
+            in_ = live["h", g, t, gr][:].rearrange("p (u e m) -> p u m e", u=2, e=2)
+            if eng == "s":
+                nc.scalar.activation(out=out, in_=in_, func=ACT.Copy, scale=c_f32[:, g, t : t + 1])
+            else:
+                nc.vector.tensor_scalar(out=out, in0=in_, scalar1=c_f32[:, g, t : t + 1], scalar2=None, op0=ALU.mult)
+
+        def h_weave(g, gr, u, eng):
+            if u == 0:
+                live["g1", g, gr] = ring.tile([P, PACK * G], BF16, name="g1", bufs=4, align_bytes=64)
+            copy_on(
+                eng,
+                live["g1", g, gr][:].rearrange("p (e u mh ml t) -> p u mh t ml e", e=2, u=2, ml=2, t=PACK)[:, u],
+                ht[g, gr][:].rearrange("p (t u mh ml e) -> p u mh t ml e", e=2, u=2, ml=2, t=PACK)[:, u],
+            )
+
+        def h1_q(g, gr):
+            quantize(h1q[g, gr], slice(0, G), live["g1", g, gr][:])
+
+        def h_turn(g, gr, half):
+            bank = new_bank()
+            words = ht[g, gr][:].bitcast(F32)
+            for s in range(4):
+                lo = (4 * half + s) * P
+                nc.tensor.transpose(bank[:, s * P : (s + 1) * P], words[:, lo : lo + P], ident[:])
+            live["th", g, gr, half] = bank
+
+        def h_turn_out(g, gr, half, eng):
+            if half == 0:
+                live["g0", g, gr] = ring.tile([P, PACK * G], BF16, name="g0", bufs=4, align_bytes=64)
+            g0 = live["g0", g, gr]
+            copy_on(
+                eng,
+                g0[:].bitcast(F32).rearrange("q (p h b u) -> q h p b u", h=2, b=2, u=2)[:, half],
+                live["th", g, gr, half][:].rearrange("q (b u p) -> q p b u", b=2, u=2),
+            )
+
+        def h0_q(g, gr):
+            quantize(h0q[g, gr], slice(0, G), live["g0", g, gr][:])
+
+        e_rows = out_0.rearrange("(g m t) j -> g t m j", g=2, t=PACK)
+        v_rows = out_1.rearrange("(g m u e) n -> g u m e n", g=2, u=2, e=2)
+
+        def e_mm(gi, t, g):
+            bank = new_bank()
+            mx(bank, f_cols(gi, t), [fp8(h0q[g, kg], slice(0, G)) for kg in range(2)])
+            live["e", gi, t, g] = bank
+
+        def e_out(gi, t, g):
+            if ("e_res", gi, t) not in live:
+                live["e_res", gi, t] = keep.tile([P, N], F32, name="e_res%d%d" % (gi, t))
+            res = live["e_res", gi, t][:, g * G : (g + 1) * G]
+            nc.vector.tensor_tensor(out=res, in0=live["e", gi, t, g][:], in1=w_all[:, g * G : (g + 1) * G], op=ALU.mult)
+            if gi == g:
+                diag = res.rearrange("m (n t) -> m t n", t=PACK)[:, t]
+                nc.gpsimd.tensor_tensor(out=diag, in0=diag, in1=ident[:], op=ALU.subtract)
+
+        def e_store(gi, t, lo, hi):
+            nc.sync.dma_start(out=e_rows[gi, t, :, lo * G : hi * G], in_=live["e_res", gi, t][:, lo * G : hi * G])
+
+        def v_mm(gr, u, e):
+            bank = new_bank()
+            s = 2 * e + u
+            mx(
+                bank,
+                [fp8(h1q[g, gr], slice(s * P, (s + 1) * P)) for g in range(2)],
+                [(y_codes[:, g, :].bitcast(FP4X4), y_sc[:, g, :]) for g in range(2)],
+            )
+            live["v", gr, u, e] = bank
+
+        def v_out(gr, u, e):
+            if e == 0:
+                live["v_res", gr, u] = ring.tile([P, 2, C], F32, name="v_res", bufs=4)
+            nc.scalar.copy(out=live["v_res", gr, u][:, e, :], in_=live["v", gr, u, e][:])
+
+        def v_store(gr, u):
+            nc.sync.dma_start(out=v_rows[gr, u], in_=live["v_res", gr, u][:])
+
+
+        def rows_in(x, g, t, eng):
+            turn(x, g, t)
+            turn_out(x, g, t, eng)
+
+        def h_block(g, gr, engs):
+            for t in range(PACK):
+                h_mm(g, t, gr)
+                h_out(g, t, gr, engs[t])
+
+        def h_turn_block(g, gr, engs):
+            for half in range(2):
+                h_turn(g, gr, half)
+                h_turn_out(g, gr, half, engs[half])
+
+        def e_tile(gi, t, g):
+            e_mm(gi, t, g)
+            e_out(gi, t, g)
+
+        def v_pair(gr, u):
+            for e in range(2):
+                v_mm(gr, u, e)
+                v_out(gr, u, e)
+            v_store(gr, u)
+
+
+        for t in range(PACK):
+            rows_in("a", 0, t, "s")
+            turn_q("a", 0, t)
+        for t in range(PACK):
+            rows_in("f", 0, t, "s")
+            turn_q("f", 0, t)
+            if t >= 2:
+                sort_words("a", 1, 2 * t - 4)
+                sort_words("a", 1, 2 * t - 3)
+        h_block(0, 0, "ssvs")
+        for t in range(PACK):
+            rows_in("a", 1, t, "svss"[t])
+        for t in range(PACK):
+            turn_q("a", 1, t)
+        for t in range(PACK):
+            rows_in("f", 1, t, "svss"[t])
+        for t in range(PACK):
+            turn_q("f", 1, t)
+
+        def h_tile(g, t, gr):
+            h_mm(g, t, gr)
+            h_out(g, t, gr, "s")
+
+        h_weave(0, 0, 0, "v")
+        h_weave(0, 0, 1, "v")
+        h_block(0, 1, "ssss")
+        h1_q(0, 0)
+        h_turn_block(0, 0, "ss")
+        h_weave(0, 1, 0, "v")
+        h_weave(0, 1, 1, "v")
+        h_mm(1, 0, 0)
+        h_mm(1, 1, 0)
+        h0_q(0, 0)
+        h_turn_block(0, 1, "vs")
+        h0_q(0, 1)
+        h_out(1, 0, 0, "s")
+        h_out(1, 1, 0, "s")
+        h1_q(0, 1)
+        h_tile(1, 2, 0)
+        h_tile(1, 3, 0)
+        h_tile(1, 0, 1)
+        h_tile(1, 1, 1)
+        e_tile(0, 0, 0)
+        e_tile(0, 1, 0)
+        e_store(0, 0, 0, 1)
+        e_store(0, 1, 0, 1)
+        h_weave(1, 0, 0, "v")
+        h_weave(1, 0, 1, "v")
+        h_tile(1, 2, 1)
+        h_tile(1, 3, 1)
+        e_tile(0, 2, 0)
+        h1_q(1, 0)
+        e_tile(0, 3, 0)
+        e_store(0, 2, 0, 1)
+        e_store(0, 3, 0, 1)
+        h_turn_block(1, 0, "sv")
+        h_turn_block(1, 1, "sv")
+        h0_q(1, 0)
+        h0_q(1, 1)
+        v_pair(0, 0)
+        v_pair(0, 1)
+        e_tile(1, 0, 0)
+        e_store(1, 0, 0, 1)
+        h_weave(1, 1, 0, "s")
+        e_tile(1, 0, 1)
+        e_tile(0, 0, 1)
+        e_store(0, 0, 1, 2)
+        h_weave(1, 1, 1, "s")
+        e_tile(1, 1, 1)
+        e_store(1, 0, 1, 2)
+        e_tile(0, 1, 1)
+        e_store(0, 1, 1, 2)
+        h1_q(1, 1)
+        e_tile(1, 1, 0)
+        e_tile(1, 2, 1)
+        e_store(1, 1, 0, 2)
+        e_tile(1, 2, 0)
+        e_tile(1, 3, 1)
+        e_store(1, 2, 0, 2)
+        v_pair(1, 0)
+        e_tile(1, 3, 0)
+        e_store(1, 3, 0, 2)
+        e_tile(0, 2, 1)
+        e_store(0, 2, 1, 2)
+        v_pair(1, 1)
+        e_tile(0, 3, 1)
+        e_store(0, 3, 1, 2)

@@ -17,58 +17,61 @@ ALU = mybir.AluOpType
 ACT = mybir.ActivationFunctionType
 
 P = 128
-PACK = 4
-G = 512
+SLOTS = 4
+HALF = P * SLOTS
 BANKS = 8
+LINE = 4
+STAGE_BUFS = 6
+SCALAR, VECTOR = "scalar", "vector"
 
 
 def tile_split_preconditioned_operator_s8_kernel(tc, finv, a, c, w, y_words, y_scales, out_0, out_1):
     nc = tc.nc
+    halves, slots = range(2), range(SLOTS)
     with ExitStack() as ctx:
         keep = ctx.enter_context(tc.tile_pool(name="keep", bufs=1))
         ring = ctx.enter_context(tc.tile_pool(name="ring", bufs=4))
         psum = ctx.enter_context(tc.psum_pool(name="psum", bufs=1))
         ctx.enter_context(tc.manual_schedule())
 
-        used = [0]
+        banks_taken = []
+        held = {}
 
         def new_bank():
-            n = used.pop()
-            used.append(n + 1)
-            return psum.tile([P, G], F32, name="bank%d" % (n % BANKS))
+            banks_taken.append(None)
+            return psum.tile([P, HALF], F32, name="bank%d" % ((len(banks_taken) - 1) % BANKS))
 
-        def planes(name, width):
+        def mx_operand(name, width):
             codes = keep.tile([P, width], U32, name=name + "_codes", align_bytes=64)
             scales = keep.tile([P, width], U8, name=name + "_scales", align_bytes=64)
             return codes, scales
 
-        src = {"a": a, "f": finv}
-        raw = {}
+        matrices = {"a": a, "f": finv}
+        pairs = {}
 
-        def load(x, g, t0, nt):
-            tile = keep.tile([P, nt * N], BF16, name="raw_%s%d%d" % (x, g, t0), align_bytes=64)
-            rows = src[x].rearrange("(g m t) k -> g m (t k)", g=2, t=PACK)
-            nc.sync.dma_start(out=tile[:], in_=rows[g, :, t0 * N : (t0 + nt) * N])
-            for t in range(nt):
-                raw[x, g, t0 + t] = tile[:, t * N : (t + 1) * N].bitcast(F32)
+        def load_rows(x, half, slot0, count):
+            tile = keep.tile([P, count * N], BF16, name="raw_%s%d%d" % (x, half, slot0), align_bytes=64)
+            rows = matrices[x].rearrange("(g m t) k -> g m (t k)", g=2, t=SLOTS)
+            nc.sync.dma_start(out=tile[:], in_=rows[half, :, slot0 * N : (slot0 + count) * N])
+            for s in range(count):
+                pairs[x, half, slot0 + s] = tile[:, s * N : (s + 1) * N].bitcast(F32)
 
         ident = keep.tile([P, P], F32, name="ident")
         make_identity(nc, ident[:])
-        c_bf = keep.tile([P, 2, PACK], BF16, name="c_bf")
-        c_f32 = keep.tile([P, 2, PACK], F32, name="c_f32")
+        c_bf = keep.tile([P, 2, SLOTS], BF16, name="c_bf")
+        c_f32 = keep.tile([P, 2, SLOTS], F32, name="c_f32")
         w_all = keep.tile([P, N], BF16, name="w_all")
         y_codes = keep.tile([P, 2, 2 * C], U8, name="y_codes", align_bytes=64)
         y_sc = keep.tile([P, 2, C], U8, name="y_sc", align_bytes=64)
         nc.vector.memset(y_sc[:].bitcast(I32), 0)
 
-        nc.scalar.dma_start(out=c_bf[:], in_=c.rearrange("(g p t) -> p g t", g=2, t=PACK))
-        for t in range(PACK):
-            load("a", 0, t, 1)
-        for t in range(PACK):
-            load("f", 0, t, 1)
+        nc.scalar.dma_start(out=c_bf[:], in_=c.rearrange("(g p t) -> p g t", g=2, t=SLOTS))
         for x in ("a", "f"):
-            load(x, 1, 0, 2)
-            load(x, 1, 2, 2)
+            for slot in slots:
+                load_rows(x, 0, slot, 1)
+        for x in ("a", "f"):
+            load_rows(x, 1, 0, 2)
+            load_rows(x, 1, 2, 2)
         nc.sync.dma_start(out=w_all[:], in_=w.partition_broadcast(P))
         nc.sync.dma_start(out=y_codes[:].bitcast(I32), in_=y_words.rearrange("g p n -> p g n").bitcast(I32))
         for q in range(4):
@@ -78,266 +81,249 @@ def tile_split_preconditioned_operator_s8_kernel(tc, finv, a, c, w, y_words, y_s
             )
         nc.vector.tensor_copy(out=c_f32[:], in_=c_bf[:])
 
-        fq = {(g, t): planes("fq%d%d" % (g, t), 2 * P) for g in range(2) for t in range(PACK)}
-        aq = {(g, kg): planes("aq%d%d" % (g, kg), G) for g in range(2) for kg in range(2)}
-        h0q = {(g, gr): planes("h0q%d%d" % (g, gr), G) for g in range(2) for gr in range(2)}
-        h1q = {(g, gr): planes("h1q%d%d" % (g, gr), G) for g in range(2) for gr in range(2)}
-        ht = {(g, gr): keep.tile([P, PACK * G], BF16, name="ht%d%d" % (g, gr), align_bytes=64) for g in range(2) for gr in range(2)}
-        live = {}
+        f_q = {(g, t): mx_operand("fq%d%d" % (g, t), 2 * P) for g in halves for t in slots}
+        a_q = {(g, kp): mx_operand("aq%d%d" % (g, kp), HALF) for g in halves for kp in halves}
+        h_for_e = {(jh, rh): mx_operand("he%d%d" % (jh, rh), HALF) for jh in halves for rh in halves}
+        h_for_v = {(jh, rh): mx_operand("hv%d%d" % (jh, rh), HALF) for jh in halves for rh in halves}
+        h_t = {
+            (jh, rh): keep.tile([P, SLOTS * HALF], BF16, name="ht%d%d" % (jh, rh), align_bytes=64)
+            for jh in halves
+            for rh in halves
+        }
 
-        def copy_on(eng, out, in_):
-            if eng == "s":
+        def copy_on(engine, out, in_):
+            if engine == SCALAR:
                 nc.scalar.copy(out=out, in_=in_)
             else:
                 nc.vector.tensor_copy(out=out, in_=in_)
 
-        def quantize(dst, cols, in_):
-            nc.vector.quantize_mx(out=dst[0][:, cols].bitcast(FP8X4), scales=dst[1][:, cols], in_=in_)
+        def quantize(operand, cols, in_):
+            nc.vector.quantize_mx(out=operand[0][:, cols].bitcast(FP8X4), scales=operand[1][:, cols], in_=in_)
 
-        def sort_words(x, g, t):
-            tile = ring.tile([P, G], F32, name="sorted", align_bytes=64)
-            nc.vector.tensor_copy(
-                out=tile[:].rearrange("m (kg u p) -> m kg u p", kg=2, u=2),
-                in_=raw[x, g, t].rearrange("m (kg p u) -> m kg u p", kg=2, u=2),
-            )
-            live["sorted", x, g, t] = tile
+        def e4m3(operand, cols):
+            return operand[0][:, cols].bitcast(FP8X4), operand[1][:, cols]
 
-        def turn(x, g, t):
+        def product(stationary, moving):
             bank = new_bank()
-            for kg in range(2):
-                for u in range(2):
-                    s = 2 * kg + u
-                    if ("sorted", x, g, t) in live:
-                        words = live["sorted", x, g, t][:, s * P : (s + 1) * P]
-                    else:
-                        words = raw[x, g, t][:, 256 * kg + u : 256 * (kg + 1) : 2]
-                    nc.tensor.transpose(bank[:, s * P : (s + 1) * P], words, ident[:])
-            live["bank", x, g, t] = bank
-
-        def turn_out(x, g, t, eng):
-            stage = ring.tile([P, N], BF16, name="stage", align_bytes=64)
-            copy_on(
-                eng,
-                stage[:].bitcast(F32).rearrange("p (kg m u) -> p kg m u", kg=2, u=2),
-                live["bank", x, g, t][:].rearrange("p (kg u m) -> p kg m u", kg=2, u=2),
-            )
-            live["stage", x, g, t] = stage
-
-        def turn_q(x, g, t):
-            stage = live["stage", x, g, t]
-            if x == "f":
-                quantize(fq[g, t], slice(0, 2 * P), stage[:])
-            else:
-                for kg in range(2):
-                    quantize(aq[g, kg], slice(t * P, (t + 1) * P), stage[:, kg * G : (kg + 1) * G])
-
-        def mx(bank, lhs, rhs):
-            for kg in range(2):
+            for kp in halves:
                 nc.tensor.matmul_mx(
-                    out=bank[:], lhsT=lhs[kg][0], lhsT_scale=lhs[kg][1], rhs=rhs[kg][0], rhs_scale=rhs[kg][1],
-                    start=(kg == 0), stop=(kg == 1),
+                    out=bank[:],
+                    lhsT=stationary[kp][0],
+                    lhsT_scale=stationary[kp][1],
+                    rhs=moving[kp][0],
+                    rhs_scale=moving[kp][1],
+                    start=(kp == 0),
+                    stop=(kp == 1),
                 )
+            return bank
 
-        def fp8(pl, cols):
-            return pl[0][:, cols].bitcast(FP8X4), pl[1][:, cols]
+        def f_rows(half, slot):
+            return [e4m3(f_q[half, slot], slice(kp * P, (kp + 1) * P)) for kp in halves]
 
-        def f_cols(g, t):
-            return [fp8(fq[g, t], slice(kg * P, (kg + 1) * P)) for kg in range(2)]
+        def sort_pairs(x, half, slot):
+            tile = ring.tile([P, HALF], F32, name="sorted", bufs=2 * SLOTS, align_bytes=64)
+            nc.vector.tensor_copy(
+                out=tile[:].rearrange("m (kp u p i) -> m kp p u i", kp=2, u=2, i=LINE),
+                in_=pairs[x, half, slot].rearrange("m (kp p i u) -> m kp p u i", kp=2, u=2, i=LINE),
+            )
+            held["sorted", x, half, slot] = tile
 
-        def h_mm(g, t, gr):
+        def turn_rows(x, half, slot, engine):
             bank = new_bank()
-            mx(bank, f_cols(g, t), [fp8(aq[gr, kg], slice(0, G)) for kg in range(2)])
-            live["h", g, t, gr] = bank
+            for kp in halves:
+                for u in range(2):
+                    s = 2 * kp + u
+                    if ("sorted", x, half, slot) in held:
+                        source = held["sorted", x, half, slot][:, s * P : (s + 1) * P]
+                    else:
+                        source = pairs[x, half, slot][:, 2 * P * kp + u : 2 * P * (kp + 1) : 2]
+                    nc.tensor.transpose(bank[:, s * P : (s + 1) * P], source, ident[:])
+            stage = ring.tile([P, N], BF16, name="stage", bufs=STAGE_BUFS, align_bytes=64)
+            copy_on(
+                engine,
+                stage[:].bitcast(F32).rearrange("p (kp m u) -> p kp m u", kp=2, u=2),
+                bank[:].rearrange("p (kp u m) -> p kp m u", kp=2, u=2),
+            )
+            held["stage", x, half, slot] = stage
 
-        def h_out(g, t, gr, eng):
-            out = ht[g, gr][:, t * G : (t + 1) * G].rearrange("p (u m e) -> p u m e", u=2, e=2)
-            in_ = live["h", g, t, gr][:].rearrange("p (u e m) -> p u m e", u=2, e=2)
-            if eng == "s":
-                nc.scalar.activation(out=out, in_=in_, func=ACT.Copy, scale=c_f32[:, g, t : t + 1])
+        def quantize_rows(x, half, slot):
+            stage = held["stage", x, half, slot]
+            if x == "f":
+                quantize(f_q[half, slot], slice(0, 2 * P), stage[:])
             else:
-                nc.vector.tensor_scalar(out=out, in0=in_, scalar1=c_f32[:, g, t : t + 1], scalar2=None, op0=ALU.mult)
+                for kp in halves:
+                    quantize(a_q[half, kp], slice(slot * P, (slot + 1) * P), stage[:, kp * HALF : (kp + 1) * HALF])
 
-        def h_weave(g, gr, u, eng):
+        def h_product(jh, slot, rh):
+            held["h", jh, slot, rh] = product(f_rows(jh, slot), [e4m3(a_q[rh, kp], slice(0, HALF)) for kp in halves])
+
+        def h_scale(jh, slot, rh, engine):
+            out = h_t[jh, rh][:, slot * HALF : (slot + 1) * HALF].rearrange("p (u m e) -> p u m e", u=2, e=2)
+            in_ = held["h", jh, slot, rh][:].rearrange("p (u e m) -> p u m e", u=2, e=2)
+            factor = c_f32[:, jh, slot : slot + 1]
+            if engine == SCALAR:
+                nc.scalar.activation(out=out, in_=in_, func=ACT.Copy, scale=factor)
+            else:
+                nc.vector.tensor_scalar(out=out, in0=in_, scalar1=factor, scalar2=None, op0=ALU.mult)
+
+        def h_tile(jh, slot, rh, engine):
+            h_product(jh, slot, rh)
+            h_scale(jh, slot, rh, engine)
+
+        def weave(jh, rh, u, engine):
             if u == 0:
-                live["g1", g, gr] = ring.tile([P, PACK * G], BF16, name="g1", bufs=4, align_bytes=64)
+                held["woven", jh, rh] = ring.tile([P, SLOTS * HALF], BF16, name="woven", align_bytes=64)
             copy_on(
-                eng,
-                live["g1", g, gr][:].rearrange("p (e u mh ml t) -> p u mh t ml e", e=2, u=2, ml=2, t=PACK)[:, u],
-                ht[g, gr][:].rearrange("p (t u mh ml e) -> p u mh t ml e", e=2, u=2, ml=2, t=PACK)[:, u],
+                engine,
+                held["woven", jh, rh][:].rearrange("p (e u mh ml t) -> p u mh t ml e", e=2, u=2, ml=2, t=SLOTS)[:, u],
+                h_t[jh, rh][:].rearrange("p (t u mh ml e) -> p u mh t ml e", e=2, u=2, ml=2, t=SLOTS)[:, u],
             )
 
-        def h1_q(g, gr):
-            quantize(h1q[g, gr], slice(0, G), live["g1", g, gr][:])
+        def quantize_for_v(jh, rh):
+            quantize(h_for_v[jh, rh], slice(0, HALF), held["woven", jh, rh][:])
 
-        def h_turn(g, gr, half):
-            bank = new_bank()
-            words = ht[g, gr][:].bitcast(F32)
-            for s in range(4):
-                lo = (4 * half + s) * P
-                nc.tensor.transpose(bank[:, s * P : (s + 1) * P], words[:, lo : lo + P], ident[:])
-            live["th", g, gr, half] = bank
+        def turn_h(jh, rh, engines):
+            row_pairs = h_t[jh, rh][:].bitcast(F32)
+            turned = ring.tile([P, SLOTS * HALF], BF16, name="turned", align_bytes=64)
+            for b in range(2):
+                bank = new_bank()
+                for i in range(4):
+                    lo = (4 * b + i) * P
+                    nc.tensor.transpose(bank[:, i * P : (i + 1) * P], row_pairs[:, lo : lo + P], ident[:])
+                copy_on(
+                    engines[b],
+                    turned[:].bitcast(F32).rearrange("m (p b s u) -> m b p s u", b=2, s=2, u=2)[:, b],
+                    bank[:].rearrange("m (s u p) -> m p s u", s=2, u=2),
+                )
+            held["turned", jh, rh] = turned
 
-        def h_turn_out(g, gr, half, eng):
-            if half == 0:
-                live["g0", g, gr] = ring.tile([P, PACK * G], BF16, name="g0", bufs=4, align_bytes=64)
-            g0 = live["g0", g, gr]
-            copy_on(
-                eng,
-                g0[:].bitcast(F32).rearrange("q (p h b u) -> q h p b u", h=2, b=2, u=2)[:, half],
-                live["th", g, gr, half][:].rearrange("q (b u p) -> q p b u", b=2, u=2),
-            )
+        def quantize_for_e(jh, rh):
+            quantize(h_for_e[jh, rh], slice(0, HALF), held["turned", jh, rh][:])
 
-        def h0_q(g, gr):
-            quantize(h0q[g, gr], slice(0, G), live["g0", g, gr][:])
-
-        e_rows = out_0.rearrange("(g m t) j -> g t m j", g=2, t=PACK)
+        e_rows = out_0.rearrange("(g m t) j -> g t m j", g=2, t=SLOTS)
         v_rows = out_1.rearrange("(g m u e) n -> g u m e n", g=2, u=2, e=2)
 
-        def e_mm(gi, t, g):
-            bank = new_bank()
-            mx(bank, f_cols(gi, t), [fp8(h0q[g, kg], slice(0, G)) for kg in range(2)])
-            live["e", gi, t, g] = bank
+        def e_tile(ih, slot, jh):
+            bank = product(f_rows(ih, slot), [e4m3(h_for_e[jh, rh], slice(0, HALF)) for rh in halves])
+            if ("e", ih, slot) not in held:
+                held["e", ih, slot] = keep.tile([P, N], F32, name="e_res%d%d" % (ih, slot))
+            res = held["e", ih, slot][:, jh * HALF : (jh + 1) * HALF]
+            nc.vector.tensor_tensor(out=res, in0=bank[:], in1=w_all[:, jh * HALF : (jh + 1) * HALF], op=ALU.mult)
+            if ih == jh:
+                diagonal = res.rearrange("m (n t) -> m t n", t=SLOTS)[:, slot]
+                nc.gpsimd.tensor_tensor(out=diagonal, in0=diagonal, in1=ident[:], op=ALU.subtract)
 
-        def e_out(gi, t, g):
-            if ("e_res", gi, t) not in live:
-                live["e_res", gi, t] = keep.tile([P, N], F32, name="e_res%d%d" % (gi, t))
-            res = live["e_res", gi, t][:, g * G : (g + 1) * G]
-            nc.vector.tensor_tensor(out=res, in0=live["e", gi, t, g][:], in1=w_all[:, g * G : (g + 1) * G], op=ALU.mult)
-            if gi == g:
-                diag = res.rearrange("m (n t) -> m t n", t=PACK)[:, t]
-                nc.gpsimd.tensor_tensor(out=diag, in0=diag, in1=ident[:], op=ALU.subtract)
+        def e_store(ih, slot, cols):
+            nc.sync.dma_start(out=e_rows[ih, slot, :, cols], in_=held["e", ih, slot][:, cols])
 
-        def e_store(gi, t, lo, hi):
-            nc.sync.dma_start(out=e_rows[gi, t, :, lo * G : hi * G], in_=live["e_res", gi, t][:, lo * G : hi * G])
+        left, right, whole = slice(0, HALF), slice(HALF, N), slice(0, N)
 
-        def v_mm(gr, u, e):
-            bank = new_bank()
-            s = 2 * e + u
-            mx(
-                bank,
-                [fp8(h1q[g, gr], slice(s * P, (s + 1) * P)) for g in range(2)],
-                [(y_codes[:, g, :].bitcast(FP4X4), y_sc[:, g, :]) for g in range(2)],
-            )
-            live["v", gr, u, e] = bank
+        def e_tile_out(ih, slot, jh):
+            e_tile(ih, slot, jh)
+            e_store(ih, slot, (left, right)[jh])
 
-        def v_out(gr, u, e):
-            if e == 0:
-                live["v_res", gr, u] = ring.tile([P, 2, C], F32, name="v_res", bufs=4)
-            nc.scalar.copy(out=live["v_res", gr, u][:, e, :], in_=live["v", gr, u, e][:])
-
-        def v_store(gr, u):
-            nc.sync.dma_start(out=v_rows[gr, u], in_=live["v_res", gr, u][:])
-
-
-        def rows_in(x, g, t, eng):
-            turn(x, g, t)
-            turn_out(x, g, t, eng)
-
-        def h_block(g, gr, engs):
-            for t in range(PACK):
-                h_mm(g, t, gr)
-                h_out(g, t, gr, engs[t])
-
-        def h_turn_block(g, gr, engs):
-            for half in range(2):
-                h_turn(g, gr, half)
-                h_turn_out(g, gr, half, engs[half])
-
-        def e_tile(gi, t, g):
-            e_mm(gi, t, g)
-            e_out(gi, t, g)
-
-        def v_pair(gr, u):
+        def v_pair_out(rh, u):
+            res = ring.tile([P, 2, C], F32, name="v_res")
             for e in range(2):
-                v_mm(gr, u, e)
-                v_out(gr, u, e)
-            v_store(gr, u)
+                cols = slice((2 * e + u) * P, (2 * e + u + 1) * P)
+                bank = product(
+                    [e4m3(h_for_v[jh, rh], cols) for jh in halves],
+                    [(y_codes[:, jh, :].bitcast(FP4X4), y_sc[:, jh, :]) for jh in halves],
+                )
+                nc.scalar.copy(out=res[:, e, :], in_=bank[:])
+            nc.sync.dma_start(out=v_rows[rh, u], in_=res[:])
 
+        for slot in slots:
+            turn_rows("a", 0, slot, SCALAR)
+            quantize_rows("a", 0, slot)
+        for slot in (0, 1):
+            turn_rows("f", 0, slot, SCALAR)
+            quantize_rows("f", 0, slot)
+        for slot in (2, 3):
+            if slot == 2:
+                sort_pairs("a", 1, 0)
+                sort_pairs("a", 1, 1)
+            turn_rows("f", 0, slot, SCALAR)
+            if slot == 3:
+                sort_pairs("a", 1, 2)
+                sort_pairs("a", 1, 3)
+            quantize_rows("f", 0, slot)
 
-        for t in range(PACK):
-            rows_in("a", 0, t, "s")
-            turn_q("a", 0, t)
-        for t in range(PACK):
-            rows_in("f", 0, t, "s")
-            turn_q("f", 0, t)
-            if t >= 2:
-                sort_words("a", 1, 2 * t - 4)
-                sort_words("a", 1, 2 * t - 3)
-        h_block(0, 0, "ssvs")
-        for t in range(PACK):
-            rows_in("a", 1, t, "svss"[t])
-        for t in range(PACK):
-            turn_q("a", 1, t)
-        for t in range(PACK):
-            rows_in("f", 1, t, "svss"[t])
-        for t in range(PACK):
-            turn_q("f", 1, t)
+        for slot in (0, 1):
+            h_tile(0, slot, 0, SCALAR)
+        for slot in slots:
+            turn_rows("a", 1, slot, SCALAR)
+        for first in (0, 2):
+            sort_pairs("f", 1, first)
+            sort_pairs("f", 1, first + 1)
+            if first == 2:
+                h_product(0, 2, 0)
+                h_product(0, 3, 0)
+            quantize_rows("a", 1, first)
+            quantize_rows("a", 1, first + 1)
+        h_scale(0, 2, 0, SCALAR)
+        h_scale(0, 3, 0, VECTOR)
+        for slot in slots:
+            turn_rows("f", 1, slot, VECTOR if slot == 1 else SCALAR)
+        for slot in slots:
+            quantize_rows("f", 1, slot)
 
-        def h_tile(g, t, gr):
-            h_mm(g, t, gr)
-            h_out(g, t, gr, "s")
+        weave(0, 0, 0, VECTOR)
+        weave(0, 0, 1, VECTOR)
+        for slot in slots:
+            h_tile(0, slot, 1, SCALAR)
+        quantize_for_v(0, 0)
+        weave(0, 1, 0, VECTOR)
+        h_tile(1, 0, 0, SCALAR)
+        h_product(1, 1, 0)
+        turn_h(0, 0, (SCALAR, SCALAR))
+        turn_h(0, 1, (VECTOR, SCALAR))
+        weave(0, 1, 1, VECTOR)
+        quantize_for_e(0, 0)
+        quantize_for_e(0, 1)
+        h_scale(1, 1, 0, SCALAR)
+        quantize_for_v(0, 1)
+        for slot in (2, 3):
+            h_tile(1, slot, 0, SCALAR)
+        for slot in (0, 1):
+            h_tile(1, slot, 1, SCALAR)
 
-        h_weave(0, 0, 0, "v")
-        h_weave(0, 0, 1, "v")
-        h_block(0, 1, "ssss")
-        h1_q(0, 0)
-        h_turn_block(0, 0, "ss")
-        h_weave(0, 1, 0, "v")
-        h_weave(0, 1, 1, "v")
-        h_mm(1, 0, 0)
-        h_mm(1, 1, 0)
-        h0_q(0, 0)
-        h_turn_block(0, 1, "vs")
-        h0_q(0, 1)
-        h_out(1, 0, 0, "s")
-        h_out(1, 1, 0, "s")
-        h1_q(0, 1)
-        h_tile(1, 2, 0)
-        h_tile(1, 3, 0)
-        h_tile(1, 0, 1)
-        h_tile(1, 1, 1)
+        weave(1, 0, 0, VECTOR)
+        weave(1, 0, 1, VECTOR)
         e_tile(0, 0, 0)
+        e_tile_out(1, 0, 0)
+        e_store(0, 0, left)
+        h_tile(1, 2, 1, SCALAR)
+        h_tile(1, 3, 1, VECTOR)
+        quantize_for_v(1, 0)
         e_tile(0, 1, 0)
-        e_store(0, 0, 0, 1)
-        e_store(0, 1, 0, 1)
-        h_weave(1, 0, 0, "v")
-        h_weave(1, 0, 1, "v")
-        h_tile(1, 2, 1)
-        h_tile(1, 3, 1)
-        e_tile(0, 2, 0)
-        h1_q(1, 0)
-        e_tile(0, 3, 0)
-        e_store(0, 2, 0, 1)
-        e_store(0, 3, 0, 1)
-        h_turn_block(1, 0, "sv")
-        h_turn_block(1, 1, "sv")
-        h0_q(1, 0)
-        h0_q(1, 1)
-        v_pair(0, 0)
-        v_pair(0, 1)
-        e_tile(1, 0, 0)
-        e_store(1, 0, 0, 1)
-        h_weave(1, 1, 0, "s")
+        e_tile_out(1, 1, 0)
+        e_store(0, 1, left)
+        turn_h(1, 0, (SCALAR, VECTOR))
+        turn_h(1, 1, (SCALAR, SCALAR))
+        quantize_for_e(1, 0)
+        quantize_for_e(1, 1)
+
+        for u in range(2):
+            v_pair_out(0, u)
+        for u in range(2):
+            weave(1, 1, u, SCALAR)
+        for slot in (2, 3):
+            e_tile(0, slot, 0)
+            e_tile_out(1, slot, 0)
+        for slot in (2, 3):
+            e_tile(0, slot, 1)
+            e_store(0, slot, whole)
+        quantize_for_v(1, 1)
         e_tile(1, 0, 1)
-        e_tile(0, 0, 1)
-        e_store(0, 0, 1, 2)
-        h_weave(1, 1, 1, "s")
+        e_tile_out(0, 0, 1)
+        e_store(1, 0, right)
         e_tile(1, 1, 1)
-        e_store(1, 0, 1, 2)
-        e_tile(0, 1, 1)
-        e_store(0, 1, 1, 2)
-        h1_q(1, 1)
-        e_tile(1, 1, 0)
+        v_pair_out(1, 0)
+        e_store(1, 1, right)
         e_tile(1, 2, 1)
-        e_store(1, 1, 0, 2)
-        e_tile(1, 2, 0)
         e_tile(1, 3, 1)
-        e_store(1, 2, 0, 2)
-        v_pair(1, 0)
-        e_tile(1, 3, 0)
-        e_store(1, 3, 0, 2)
-        e_tile(0, 2, 1)
-        e_store(0, 2, 1, 2)
-        v_pair(1, 1)
-        e_tile(0, 3, 1)
-        e_store(0, 3, 1, 2)
+        e_store(1, 2, right)
+        v_pair_out(1, 1)
+        e_store(1, 3, right)
+        e_tile_out(0, 1, 1)

from contextlib import ExitStack

import concourse.mybir as mybir
from concourse.masks import make_identity

N, C = 1024, 512
FLOPS = 2 * N * N * N * 2 + 2 * N * N * C

F32 = mybir.dt.float32
BF16 = mybir.dt.bfloat16
U32 = mybir.dt.uint32
I32 = mybir.dt.int32
U8 = mybir.dt.uint8
FP8X4 = mybir.dt.float8_e4m3fn_x4
FP4X4 = mybir.dt.float4_e2m1fn_x4
ALU = mybir.AluOpType
ACT = mybir.ActivationFunctionType

P = 128
SLOTS = 4
HALF = P * SLOTS
BANKS = 8
LINE = 4
STAGE_BUFS = 6
SCALAR, VECTOR = "scalar", "vector"


def tile_split_preconditioned_operator_s8_kernel(tc, finv, a, c, w, y_words, y_scales, out_0, out_1):
    nc = tc.nc
    halves, slots = range(2), range(SLOTS)
    with ExitStack() as ctx:
        keep = ctx.enter_context(tc.tile_pool(name="keep", bufs=1))
        ring = ctx.enter_context(tc.tile_pool(name="ring", bufs=4))
        psum = ctx.enter_context(tc.psum_pool(name="psum", bufs=1))
        ctx.enter_context(tc.manual_schedule())

        banks_taken = []
        held = {}

        def new_bank():
            banks_taken.append(None)
            return psum.tile([P, HALF], F32, name="bank%d" % ((len(banks_taken) - 1) % BANKS))

        def mx_operand(name, width):
            codes = keep.tile([P, width], U32, name=name + "_codes", align_bytes=64)
            scales = keep.tile([P, width], U8, name=name + "_scales", align_bytes=64)
            return codes, scales

        matrices = {"a": a, "f": finv}
        pairs = {}

        def load_rows(x, half, slot0, count):
            tile = keep.tile([P, count * N], BF16, name="raw_%s%d%d" % (x, half, slot0), align_bytes=64)
            rows = matrices[x].rearrange("(g m t) k -> g m (t k)", g=2, t=SLOTS)
            nc.sync.dma_start(out=tile[:], in_=rows[half, :, slot0 * N : (slot0 + count) * N])
            for s in range(count):
                pairs[x, half, slot0 + s] = tile[:, s * N : (s + 1) * N].bitcast(F32)

        ident = keep.tile([P, P], F32, name="ident")
        make_identity(nc, ident[:])
        c_bf = keep.tile([P, 2, SLOTS], BF16, name="c_bf")
        c_f32 = keep.tile([P, 2, SLOTS], F32, name="c_f32")
        w_all = keep.tile([P, N], BF16, name="w_all")
        y_codes = keep.tile([P, 2, 2 * C], U8, name="y_codes", align_bytes=64)
        y_sc = keep.tile([P, 2, C], U8, name="y_sc", align_bytes=64)
        nc.vector.memset(y_sc[:].bitcast(I32), 0)

        nc.scalar.dma_start(out=c_bf[:], in_=c.rearrange("(g p t) -> p g t", g=2, t=SLOTS))
        for x in ("a", "f"):
            for slot in slots:
                load_rows(x, 0, slot, 1)
        for x in ("a", "f"):
            load_rows(x, 1, 0, 2)
            load_rows(x, 1, 2, 2)
        nc.sync.dma_start(out=w_all[:], in_=w.partition_broadcast(P))
        nc.sync.dma_start(out=y_codes[:].bitcast(I32), in_=y_words.rearrange("g p n -> p g n").bitcast(I32))
        for q in range(4):
            nc.sync.dma_start(
                out=y_sc[32 * q : 32 * q + 4].bitcast(I32),
                in_=y_scales[:, 4 * q : 4 * q + 4, :].rearrange("g r n -> r g n").bitcast(I32),
            )
        nc.vector.tensor_copy(out=c_f32[:], in_=c_bf[:])

        f_q = {(g, t): mx_operand("fq%d%d" % (g, t), 2 * P) for g in halves for t in slots}
        a_q = {(g, kp): mx_operand("aq%d%d" % (g, kp), HALF) for g in halves for kp in halves}
        h_for_e = {(jh, rh): mx_operand("he%d%d" % (jh, rh), HALF) for jh in halves for rh in halves}
        h_for_v = {(jh, rh): mx_operand("hv%d%d" % (jh, rh), HALF) for jh in halves for rh in halves}
        h_t = {
            (jh, rh): keep.tile([P, SLOTS * HALF], BF16, name="ht%d%d" % (jh, rh), align_bytes=64)
            for jh in halves
            for rh in halves
        }

        def copy_on(engine, out, in_):
            if engine == SCALAR:
                nc.scalar.copy(out=out, in_=in_)
            else:
                nc.vector.tensor_copy(out=out, in_=in_)

        def quantize(operand, cols, in_):
            nc.vector.quantize_mx(out=operand[0][:, cols].bitcast(FP8X4), scales=operand[1][:, cols], in_=in_)

        def e4m3(operand, cols):
            return operand[0][:, cols].bitcast(FP8X4), operand[1][:, cols]

        def product(stationary, moving):
            bank = new_bank()
            for kp in halves:
                nc.tensor.matmul_mx(
                    out=bank[:],
                    lhsT=stationary[kp][0],
                    lhsT_scale=stationary[kp][1],
                    rhs=moving[kp][0],
                    rhs_scale=moving[kp][1],
                    start=(kp == 0),
                    stop=(kp == 1),
                )
            return bank

        def f_rows(half, slot):
            return [e4m3(f_q[half, slot], slice(kp * P, (kp + 1) * P)) for kp in halves]

        def sort_pairs(x, half, slot):
            tile = ring.tile([P, HALF], F32, name="sorted", bufs=2 * SLOTS, align_bytes=64)
            nc.vector.tensor_copy(
                out=tile[:].rearrange("m (kp u p i) -> m kp p u i", kp=2, u=2, i=LINE),
                in_=pairs[x, half, slot].rearrange("m (kp p i u) -> m kp p u i", kp=2, u=2, i=LINE),
            )
            held["sorted", x, half, slot] = tile

        def turn_rows(x, half, slot, engine):
            bank = new_bank()
            for kp in halves:
                for u in range(2):
                    s = 2 * kp + u
                    if ("sorted", x, half, slot) in held:
                        source = held["sorted", x, half, slot][:, s * P : (s + 1) * P]
                    else:
                        source = pairs[x, half, slot][:, 2 * P * kp + u : 2 * P * (kp + 1) : 2]
                    nc.tensor.transpose(bank[:, s * P : (s + 1) * P], source, ident[:])
            stage = ring.tile([P, N], BF16, name="stage", bufs=STAGE_BUFS, align_bytes=64)
            copy_on(
                engine,
                stage[:].bitcast(F32).rearrange("p (kp m u) -> p kp m u", kp=2, u=2),
                bank[:].rearrange("p (kp u m) -> p kp m u", kp=2, u=2),
            )
            held["stage", x, half, slot] = stage

        def quantize_rows(x, half, slot):
            stage = held["stage", x, half, slot]
            if x == "f":
                quantize(f_q[half, slot], slice(0, 2 * P), stage[:])
            else:
                for kp in halves:
                    quantize(a_q[half, kp], slice(slot * P, (slot + 1) * P), stage[:, kp * HALF : (kp + 1) * HALF])

        def h_product(jh, slot, rh):
            held["h", jh, slot, rh] = product(f_rows(jh, slot), [e4m3(a_q[rh, kp], slice(0, HALF)) for kp in halves])

        def h_scale(jh, slot, rh, engine):
            out = h_t[jh, rh][:, slot * HALF : (slot + 1) * HALF].rearrange("p (u m e) -> p u m e", u=2, e=2)
            in_ = held["h", jh, slot, rh][:].rearrange("p (u e m) -> p u m e", u=2, e=2)
            factor = c_f32[:, jh, slot : slot + 1]
            if engine == SCALAR:
                nc.scalar.activation(out=out, in_=in_, func=ACT.Copy, scale=factor)
            else:
                nc.vector.tensor_scalar(out=out, in0=in_, scalar1=factor, scalar2=None, op0=ALU.mult)

        def h_tile(jh, slot, rh, engine):
            h_product(jh, slot, rh)
            h_scale(jh, slot, rh, engine)

        def weave(jh, rh, u, engine):
            if u == 0:
                held["woven", jh, rh] = ring.tile([P, SLOTS * HALF], BF16, name="woven", align_bytes=64)
            copy_on(
                engine,
                held["woven", jh, rh][:].rearrange("p (e u mh ml t) -> p u mh t ml e", e=2, u=2, ml=2, t=SLOTS)[:, u],
                h_t[jh, rh][:].rearrange("p (t u mh ml e) -> p u mh t ml e", e=2, u=2, ml=2, t=SLOTS)[:, u],
            )

        def quantize_for_v(jh, rh):
            quantize(h_for_v[jh, rh], slice(0, HALF), held["woven", jh, rh][:])

        def turn_h(jh, rh, engines):
            row_pairs = h_t[jh, rh][:].bitcast(F32)
            turned = ring.tile([P, SLOTS * HALF], BF16, name="turned", align_bytes=64)
            for b in range(2):
                bank = new_bank()
                for i in range(4):
                    lo = (4 * b + i) * P
                    nc.tensor.transpose(bank[:, i * P : (i + 1) * P], row_pairs[:, lo : lo + P], ident[:])
                copy_on(
                    engines[b],
                    turned[:].bitcast(F32).rearrange("m (p b s u) -> m b p s u", b=2, s=2, u=2)[:, b],
                    bank[:].rearrange("m (s u p) -> m p s u", s=2, u=2),
                )
            held["turned", jh, rh] = turned

        def quantize_for_e(jh, rh):
            quantize(h_for_e[jh, rh], slice(0, HALF), held["turned", jh, rh][:])

        e_rows = out_0.rearrange("(g m t) j -> g t m j", g=2, t=SLOTS)
        v_rows = out_1.rearrange("(g m u e) n -> g u m e n", g=2, u=2, e=2)

        def e_tile(ih, slot, jh):
            bank = product(f_rows(ih, slot), [e4m3(h_for_e[jh, rh], slice(0, HALF)) for rh in halves])
            if ("e", ih, slot) not in held:
                held["e", ih, slot] = keep.tile([P, N], F32, name="e_res%d%d" % (ih, slot))
            res = held["e", ih, slot][:, jh * HALF : (jh + 1) * HALF]
            nc.vector.tensor_tensor(out=res, in0=bank[:], in1=w_all[:, jh * HALF : (jh + 1) * HALF], op=ALU.mult)
            if ih == jh:
                diagonal = res.rearrange("m (n t) -> m t n", t=SLOTS)[:, slot]
                nc.gpsimd.tensor_tensor(out=diagonal, in0=diagonal, in1=ident[:], op=ALU.subtract)

        def e_store(ih, slot, cols):
            nc.sync.dma_start(out=e_rows[ih, slot, :, cols], in_=held["e", ih, slot][:, cols])

        left, right, whole = slice(0, HALF), slice(HALF, N), slice(0, N)

        def e_tile_out(ih, slot, jh):
            e_tile(ih, slot, jh)
            e_store(ih, slot, (left, right)[jh])

        def v_pair_out(rh, u):
            res = ring.tile([P, 2, C], F32, name="v_res")
            for e in range(2):
                cols = slice((2 * e + u) * P, (2 * e + u + 1) * P)
                bank = product(
                    [e4m3(h_for_v[jh, rh], cols) for jh in halves],
                    [(y_codes[:, jh, :].bitcast(FP4X4), y_sc[:, jh, :]) for jh in halves],
                )
                nc.scalar.copy(out=res[:, e, :], in_=bank[:])
            nc.sync.dma_start(out=v_rows[rh, u], in_=res[:])

        for slot in slots:
            turn_rows("a", 0, slot, SCALAR)
            quantize_rows("a", 0, slot)
        for slot in (0, 1):
            turn_rows("f", 0, slot, SCALAR)
            quantize_rows("f", 0, slot)
        for slot in (2, 3):
            if slot == 2:
                sort_pairs("a", 1, 0)
                sort_pairs("a", 1, 1)
            turn_rows("f", 0, slot, SCALAR)
            if slot == 3:
                sort_pairs("a", 1, 2)
                sort_pairs("a", 1, 3)
            quantize_rows("f", 0, slot)

        for slot in (0, 1):
            h_tile(0, slot, 0, SCALAR)
        for slot in slots:
            turn_rows("a", 1, slot, SCALAR)
        for first in (0, 2):
            sort_pairs("f", 1, first)
            sort_pairs("f", 1, first + 1)
            if first == 2:
                h_product(0, 2, 0)
                h_product(0, 3, 0)
            quantize_rows("a", 1, first)
            quantize_rows("a", 1, first + 1)
        h_scale(0, 2, 0, SCALAR)
        h_scale(0, 3, 0, VECTOR)
        for slot in slots:
            turn_rows("f", 1, slot, VECTOR if slot == 1 else SCALAR)
        for slot in slots:
            quantize_rows("f", 1, slot)

        weave(0, 0, 0, VECTOR)
        weave(0, 0, 1, VECTOR)
        for slot in slots:
            h_tile(0, slot, 1, SCALAR)
        quantize_for_v(0, 0)
        weave(0, 1, 0, VECTOR)
        h_tile(1, 0, 0, SCALAR)
        h_product(1, 1, 0)
        turn_h(0, 0, (SCALAR, SCALAR))
        turn_h(0, 1, (VECTOR, SCALAR))
        weave(0, 1, 1, VECTOR)
        quantize_for_e(0, 0)
        quantize_for_e(0, 1)
        h_scale(1, 1, 0, SCALAR)
        quantize_for_v(0, 1)
        for slot in (2, 3):
            h_tile(1, slot, 0, SCALAR)
        for slot in (0, 1):
            h_tile(1, slot, 1, SCALAR)

        weave(1, 0, 0, VECTOR)
        weave(1, 0, 1, VECTOR)
        e_tile(0, 0, 0)
        e_tile_out(1, 0, 0)
        e_store(0, 0, left)
        h_tile(1, 2, 1, SCALAR)
        h_tile(1, 3, 1, VECTOR)
        quantize_for_v(1, 0)
        e_tile(0, 1, 0)
        e_tile_out(1, 1, 0)
        e_store(0, 1, left)
        turn_h(1, 0, (SCALAR, VECTOR))
        turn_h(1, 1, (SCALAR, SCALAR))
        quantize_for_e(1, 0)
        quantize_for_e(1, 1)

        for u in range(2):
            v_pair_out(0, u)
        for u in range(2):
            weave(1, 1, u, SCALAR)
        for slot in (2, 3):
            e_tile(0, slot, 0)
            e_tile_out(1, slot, 0)
        for slot in (2, 3):
            e_tile(0, slot, 1)
            e_store(0, slot, whole)
        quantize_for_v(1, 1)
        e_tile(1, 0, 1)
        e_tile_out(0, 0, 1)
        e_store(1, 0, right)
        e_tile(1, 1, 1)
        v_pair_out(1, 0)
        e_store(1, 1, right)
        e_tile(1, 2, 1)
        e_tile(1, 3, 1)
        e_store(1, 2, right)
        v_pair_out(1, 1)
        e_store(1, 3, right)
        e_tile_out(0, 1, 1)
